import numpy as np
import ml_dtypes


def mxq(x, axis, fmt="e4m3"):
    dtype, down = {"e4m3": (ml_dtypes.float8_e4m3fn, 7), "e5m2": (ml_dtypes.float8_e5m2, 14)}[fmt]
    v = np.moveaxis(np.asarray(x, np.float32).astype(ml_dtypes.bfloat16).astype(np.float64), axis, -1)
    blocks = v.reshape(v.shape[:-1] + (-1, 32))
    amax = np.abs(blocks).max(-1, keepdims=True)
    byte = np.maximum(np.where(amax > 0, np.frexp(amax)[1] - 1 + 127, 0) - down, 1)
    scale = np.exp2(byte - 127.0)
    codes = (blocks / scale).astype(np.float32).astype(dtype).astype(np.float64)
    return np.moveaxis((codes * scale).reshape(v.shape), -1, axis)


WIDE = False


def mx_kscale(k):
    if not WIDE:
        return np.ones(k)
    levels = np.array([10, -10, 5, -5, 0])
    if k % 512:
        return np.exp2(np.random.permutation(np.resize(levels, k // 32))).repeat(32)
    a = np.empty((k // 512, 16))
    for p in range(k // 512):
        a[p, :8] = np.random.permutation(np.resize(levels, 8))
        for g in range(8):
            far = levels[np.abs(levels - a[p, g]) >= 10]
            a[p, g + 8] = far[np.random.randint(len(far))]
    return np.exp2(a.ravel()).repeat(32)


def f64(x):
    return np.asarray(x).astype(np.float64)


def striped(idx):
    return np.tile(np.asarray(idx).reshape(-1, 16).T, (8, 1)).astype(np.uint16)


def unstriped(offs):
    return offs[:16].T.reshape(-1).astype(np.int64)


def striped8(idx):
    return np.asarray(idx).reshape(8, -1, 16).transpose(0, 2, 1).reshape(128, -1).astype(np.uint16)


def unstriped8(offs):
    return offs.reshape(8, 16, -1).transpose(0, 2, 1).reshape(8, -1).astype(np.int64)


def pick8(x, idx, run):
    r = np.arange(len(x))
    return x[r[:, None], idx[r % (8 * run) // run]]


E2M1 = np.array([0.0, 0.5, 1.0, 1.5, 2.0, 3.0, 4.0, 6.0, -0.0, -0.5, -1.0, -1.5, -2.0, -3.0, -4.0, -6.0])


def pack_weight(w, fmt):
    k, n = w.shape
    w = f64(np.asarray(w, np.float32).astype(ml_dtypes.bfloat16)).reshape(k // 32, 32, n)
    amax = np.abs(w).max(1)
    if fmt == "e4m3":
        byte = np.frexp(amax)[1] - 1 + 127 - 7
    else:
        mant, ex = np.frexp(amax / 6.0)
        byte = np.where(mant > 0.5, ex, ex - 1) + 127
    byte = np.clip(np.where(amax > 0, byte, 1), 1, 254)
    scaled = (w * np.exp2(127.0 - byte)[:, None, :]).reshape(k, n).astype(np.float32)
    by_word = np.ascontiguousarray(scaled.reshape(k // 512, 128, 4, n).transpose(0, 1, 3, 2))
    if fmt == "e4m3":
        words = by_word.astype(ml_dtypes.float8_e4m3fn).view(np.uint8)
    else:
        c = by_word.astype(ml_dtypes.float4_e2m1fn).view(np.uint8) & 0xF
        words = (c[..., 0::2] | (c[..., 1::2] << 4)).reshape(k // 512, 128, 2 * n)
    return np.ascontiguousarray(words), np.ascontiguousarray(byte.astype(np.uint8).reshape(k // 512, 16, n))


def unpack_weight(words, scales, fmt):
    g, _, n = scales.shape
    words = np.ascontiguousarray(words).reshape(g, 128, n, -1)
    if fmt == "e4m3":
        vals = words.view(ml_dtypes.float8_e4m3fn).astype(np.float64)
    else:
        nib = np.empty((g, 128, n, 4), np.uint8)
        nib[..., 0::2] = words & 0xF
        nib[..., 1::2] = words >> 4
        vals = E2M1[nib]
    vals = vals * np.repeat(np.exp2(scales.astype(np.float64) - 127.0), 8, axis=1)[..., None]
    return vals.transpose(0, 1, 3, 2).reshape(g * 512, n)


def sgn(shape):
    return np.random.uniform(0.5, 2.0, shape) * np.where(np.random.standard_normal(shape) < 0, -1.0, 1.0)


K, J, R, T, F, O, N, S, U, E = 512, 1024, 512, 2048, 1024, 512, 256, 1024, 256, 1024


def setup_inputs():
    n = np.random.standard_normal
    idx = np.random.permutation(T)[:J]
    idx2 = np.stack([np.random.permutation(F)[:R] for _ in range(8)])
    idx3 = np.random.permutation(J)[:O]
    idx4 = np.stack([np.random.permutation(J)[:O] for _ in range(8)])
    idx5 = np.random.permutation(S)[:N]
    idx6 = np.stack([np.random.permutation(O)[:U] for _ in range(8)])
    idx7 = np.stack([np.random.permutation(E)[:U] for _ in range(8)])
    fk = mx_kscale(K)
    fr = mx_kscale(R)
    xtp = pack_weight(n((K, T)) * fk[:, None], "e2m1")
    vsp = pack_weight(n((R, S)) * 1 / np.sqrt(R) / fr[:, None], "e2m1")
    return {
        "xt_words": xtp[0],
        "xt_scales": xtp[1],
        "ua": (np.random.randint(-7, 8, (K, F)).astype(np.float64)).astype(np.float32),
        "ha": ((np.random.randint(8, 25, (K, 1)) / 1024.0) / fk[:, None]).astype(np.float32),
        "sa": (np.random.uniform(0.5, 1.6, (R, 1)) * fr[:, None]).astype(np.float32),
        "sb": (np.random.uniform(0.5, 1.6, (R, 1)) * fr[:, None]).astype(np.float32),
        "vs_words": vsp[0],
        "vs_scales": vsp[1],
        "so": (sgn((N, 1))).astype(np.float32),
        "offs": striped(idx),
        "offs2": striped8(idx2),
        "offs3": striped(idx3),
        "offs4": striped8(idx4),
        "offs5": striped(idx5),
        "offs6": striped8(idx6),
        "offs7": striped8(idx7),
    }


def reference(xt_words, xt_scales, ua, ha, sa, sb, vs_words, vs_scales, so, offs, offs2, offs3, offs4, offs5, offs6, offs7):
    idx = unstriped(offs)
    idx2 = unstriped8(offs2)
    idx3 = unstriped(offs3)
    idx4 = unstriped8(offs4)
    idx5 = unstriped(offs5)
    idx6 = unstriped8(offs6)
    idx7 = unstriped8(offs7)
    xtu = unpack_weight(xt_words, xt_scales, "e2m1")
    vsu = unpack_weight(vs_words, vs_scales, "e2m1")
    wc = pick8(f64(ua), idx2, 64) * f64(ha)
    wcq = mxq(wc, 0, "e4m3")
    xtidxg = xtu[:, idx]
    a = wcq.T @ xtidxg
    hid = np.maximum(a[:, idx3] * f64(sa), pick8(a, idx4, 64) * f64(sb))
    vsidx5g = vsu[:, idx5]
    hidq = mxq(hid, 0, "e4m3")
    p = vsidx5g.T @ hidq
    m0 = pick8(p, idx6, 16) * f64(so)
    y = np.zeros((N, E))
    y[np.arange(N)[:, None], idx7[np.arange(N) % 128 // 16]] = m0
    return y

@@ -1,0 +1,189 @@
+from contextlib import ExitStack
+
+import concourse.mybir as mybir
+
+K, J, R, T, F, O, N, S, U, E = 512, 1024, 512, 2048, 1024, 512, 256, 1024, 256, 1024
+FLOPS = 2 * K * R * J + 2 * R * N * O
+
+F32 = mybir.dt.float32
+BF16 = mybir.dt.bfloat16
+I32 = mybir.dt.int32
+U32 = mybir.dt.uint32
+U16 = mybir.dt.uint16
+U8 = mybir.dt.uint8
+FP8X4 = mybir.dt.float8_e4m3fn_x4
+FP4X4 = mybir.dt.float4_e2m1fn_x4
+COPY = mybir.ActivationFunctionType.Copy
+MAX = mybir.AluOpType.max
+
+P = 128
+PACK = 4
+BANK = 512
+LIST = 16
+
+
+def entries(offsets, lo, hi):
+    return offsets[:, lo // LIST : hi // LIST]
+
+
+def tile_picked_tokens_codes_one_mixedpair_store_posted_kernel(
+    tc, xt_words, xt_scales, ua, ha, sa, sb, vs_words, vs_scales, so,
+    offs, offs2, offs3, offs4, offs5, offs6, offs7, out,
+):
+    nc = tc.nc
+    with ExitStack() as ctx:
+        keep = ctx.enter_context(tc.tile_pool(name="keep", bufs=1))
+        psum = ctx.enter_context(tc.psum_pool(name="psum", bufs=8))
+
+        def load_list(src, name):
+            tile = keep.tile(list(src.shape), U16, name=name)
+            nc.sync.dma_start(tile[:], src)
+            return tile
+
+        def load_scale_rows(src, window, queue):
+            for q in range(4):
+                queue.dma_start(window[32 * q : 32 * q + 4, :].bitcast(I32), src[0, 4 * q : 4 * q + 4, :].bitcast(I32))
+
+        def load_dealt(src, name, queue):
+            tile = keep.tile([P, PACK], F32, name=name)
+            queue.dma_start(tile[:], src.rearrange("(p j) one -> p (j one)", j=PACK))
+            return tile
+
+        xs_win = keep.tile([P, T], U8, name="xs_win")
+        nc.vector.memset(xs_win[:].bitcast(I32), 0)
+        vs_s_win = keep.tile([P, S], U8, name="vs_s_win")
+        nc.vector.memset(vs_s_win[:].bitcast(I32), 0)
+        pages = [keep.tile([P, E], F32, name="page%d" % b) for b in range(2)]
+        for page in pages:
+            nc.vector.memset(page[:], 0.0)
+
+        list1 = load_list(offs, "list1")
+        xw_win = keep.tile([P, T], U16, name="xw_win")
+        nc.sync.dma_start(xw_win[:].bitcast(I32), xt_words[0].bitcast(I32))
+        list2 = load_list(offs2, "list2")
+        ha_t = load_dealt(ha, "ha_t", nc.sync)
+        ua_rows = ua.rearrange("(p j) f -> p j f", j=PACK)
+        ua_t = [keep.tile([P, F], F32, name="ua%d" % j) for j in range(PACK)]
+        nc.sync.dma_start(ua_t[0][:], ua_rows[:, 0, :])
+        load_scale_rows(xt_scales, xs_win, nc.sync)
+        for j in range(1, PACK):
+            nc.sync.dma_start(ua_t[j][:], ua_rows[:, j, :])
+        list4 = load_list(offs4, "list4")
+        sb_t = load_dealt(sb, "sb_t", nc.sync)
+        list3 = load_list(offs3, "list3")
+        sa_t = load_dealt(sa, "sa_t", nc.sync)
+        list5 = load_list(offs5, "list5")
+        vs_w_win = keep.tile([P, S], U16, name="vs_w_win")
+        nc.sync.dma_start(vs_w_win[:].bitcast(I32), vs_words[0].bitcast(I32))
+        load_scale_rows(vs_scales, vs_s_win, nc.sync)
+        list6 = load_list(offs6, "list6")
+        list7 = load_list(offs7, "list7")
+        so_t = keep.tile([P, 2], F32, name="so_t")
+        with nc.allow_non_contiguous_dma(reason="one weight a partition and block"):
+            nc.sync.dma_start(so_t[:], so.rearrange("(b p) one -> p (b one)", p=P))
+
+        xw = [keep.tile([P, BANK], U16, name="xw%d" % h, align_bytes=64) for h in range(2)]
+        xs = [keep.tile([P, BANK], U8, name="xs%d" % h, align_bytes=64) for h in range(2)]
+        for h in range(2):
+            nc.vector.tensor_copy(xw[h][:], xw_win[:].indirect(entries(list1, h * BANK, (h + 1) * BANK)))
+        for h in range(2):
+            nc.vector.tensor_copy(xs[h][:], xs_win[:].indirect(entries(list1, h * BANK, (h + 1) * BANK)))
+
+        wc = keep.tile([P, PACK, R], BF16, name="wc")
+        for j in range(PACK):
+            nc.scalar.activation(out=wc[:, j, :], in_=ua_t[j][:].indirect(list2[:]), func=COPY, scale=ha_t[:, j : j + 1])
+
+        wc_dealt = wc[:].rearrange("p j (m t) -> p t m j", t=PACK)
+        wc_woven = [keep.tile([P, P, PACK], BF16, name="wc_woven%d" % t, align_bytes=64) for t in range(PACK)]
+        wc_codes = [keep.tile([P, P], U32, name="wc_codes%d" % t, align_bytes=64) for t in range(PACK)]
+        wc_scales = [keep.tile([P, P], U8, name="wc_scales%d" % t, align_bytes=64) for t in range(PACK)]
+        for t in range(PACK):
+            nc.vector.tensor_copy(wc_woven[t][:], wc_dealt[:, t])
+            nc.vector.quantize_mx(
+                out=wc_codes[t][:].bitcast(FP8X4), scales=wc_scales[t][:],
+                in_=wc_woven[t][:].rearrange("p m j -> p (m j)"),
+            )
+
+        a_t = [keep.tile([P, J], F32, name="a%d" % t) for t in range(PACK)]
+        for t in range(PACK):
+            pieces = [(0, 256), (256, 512), (512, 768), (768, 1024)] if t == 0 else [(0, 512), (512, 1024)]
+            for lo, hi in pieces:
+                h, c0, c1 = lo // BANK, lo % BANK, lo % BANK + hi - lo
+                acc = psum.tile([P, BANK], F32, name="acc")
+                nc.tensor.matmul_mx(
+                    out=acc[:, : hi - lo], lhsT=wc_codes[t][:].bitcast(FP8X4), lhsT_scale=wc_scales[t][:],
+                    rhs=xw[h][:, c0:c1].bitcast(FP4X4), rhs_scale=xs[h][:, c0:c1], start=True, stop=True,
+                )
+                if t == 0:
+                    nc.scalar.copy(a_t[t][:, lo:hi], acc[:, : hi - lo])
+                else:
+                    nc.vector.tensor_copy(a_t[t][:, lo:hi], acc[:, : hi - lo])
+
+        vw = keep.tile([P, N], U16, name="vw", align_bytes=64)
+        vsc = keep.tile([P, N], U8, name="vsc", align_bytes=64)
+        nc.vector.tensor_copy(vsc[:], vs_s_win[:].indirect(list5[:]))
+        nc.vector.tensor_copy(vw[:], vs_w_win[:].indirect(list5[:]))
+
+        shared = [keep.tile([P, O], F32, name="shared%d" % t) for t in range(PACK)]
+        own = [keep.tile([P, O], F32, name="own%d" % t) for t in range(PACK)]
+        hid = keep.tile([P, PACK, O], BF16, name="hid")
+        p_t = [keep.tile([P, O], F32, name="p%d" % b) for b in range(2)]
+
+        def fetch_shared(t, lo, hi):
+            nc.scalar.activation(out=shared[t][:, lo:hi], in_=a_t[t][:].indirect(entries(list3, lo, hi)), func=COPY, scale=sa_t[:, t : t + 1])
+
+        def fetch_own(t, lo, hi):
+            nc.scalar.activation(out=own[t][:, lo:hi], in_=a_t[t][:].indirect(entries(list4, lo, hi)), func=COPY, scale=sb_t[:, t : t + 1])
+
+        def larger(t, lo, hi):
+            nc.vector.tensor_tensor(hid[:, t, lo:hi], shared[t][:, lo:hi], own[t][:, lo:hi], MAX)
+
+        sums = []
+
+        def second_product(lo, hi):
+            w = hi - lo
+            woven = keep.tile([P, w, PACK], BF16, name="hid_woven%d" % lo, align_bytes=64)
+            codes = keep.tile([P, w], U32, name="hid_codes%d" % lo, align_bytes=64)
+            scales = keep.tile([P, w], U8, name="hid_scales%d" % lo, align_bytes=64)
+            nc.vector.tensor_copy(woven[:], hid[:, :, lo:hi].rearrange("p t o -> p o t"))
+            nc.vector.quantize_mx(out=codes[:].bitcast(FP8X4), scales=scales[:], in_=woven[:].rearrange("p o t -> p (o t)"))
+            for b in range(2):
+                acc = psum.tile([P, BANK], F32, name="acc")
+                nc.tensor.matmul_mx(
+                    out=acc[:, :w], lhsT=vw[:, b * P : (b + 1) * P].bitcast(FP4X4), lhsT_scale=vsc[:, b * P : (b + 1) * P],
+                    rhs=codes[:].bitcast(FP8X4), rhs_scale=scales[:], start=True, stop=True,
+                )
+                sums.append((b, lo, hi, acc))
+
+        for t in range(2):
+            fetch_own(t, 0, O)
+            fetch_shared(t, 0, O)
+            larger(t, 0, O)
+        for t in range(2, 4):
+            fetch_own(t, 0, 256)
+            fetch_shared(t, 0, 256)
+            larger(t, 0, 256)
+        second_product(0, 256)
+        fetch_own(2, 256, 512)
+        fetch_shared(2, 256, 512)
+        larger(2, 256, 512)
+        fetch_own(3, 256, 512)
+        for lo in (256, 384):
+            fetch_shared(3, lo, lo + 128)
+            larger(3, lo, lo + 128)
+            second_product(lo, lo + 128)
+
+        for b in range(2):
+            for bb, lo, hi, acc in sums:
+                if bb == b and hi < O:
+                    nc.scalar.copy(p_t[b][:, lo:hi], acc[:, : hi - lo])
+        m0 = [keep.tile([P, U], F32, name="m0_%d" % b) for b in range(2)]
+        for b in range(2):
+            for bb, lo, hi, acc in sums:
+                if bb == b and hi == O:
+                    nc.scalar.copy(p_t[b][:, lo:hi], acc[:, : hi - lo])
+            cuts = [(0, 128), (128, 256)] if b == 0 else [(0, 256)]
+            for lo, hi in cuts:
+                nc.scalar.activation(out=m0[b][:, lo:hi], in_=p_t[b][:].indirect(entries(list6, lo, hi)), func=COPY, scale=so_t[:, b : b + 1])
+                nc.vector.tensor_copy(pages[b][:].indirect(entries(list7, lo, hi)), m0[b][:, lo:hi])
+            nc.sync.dma_start(out[b * P : (b + 1) * P, :], pages[b][:])

@@ -49,6 +49,11 @@ def tile_picked_tokens_codes_one_mixedpair_store_posted_kernel(
             queue.dma_start(tile[:], src.rearrange("(p j) one -> p (j one)", j=PACK))
             return tile
 
+        idle_in = keep.tile([P, 1], F32, name="idle_in")
+        idle_out = keep.tile([P, 1], F32, name="idle_out")
+        nc.gpsimd.memset(idle_in[:], 0.0)
+        nc.scalar.activation(out=idle_out[:], in_=idle_in[:], func=COPY)
+
         xs_win = keep.tile([P, T], U8, name="xs_win")
         nc.vector.memset(xs_win[:].bitcast(I32), 0)
         vs_s_win = keep.tile([P, S], U8, name="vs_s_win")

@@ -33,7 +33,7 @@ def tile_picked_tokens_codes_one_mixedpair_store_posted_kernel(
     nc = tc.nc
     with ExitStack() as ctx:
         keep = ctx.enter_context(tc.tile_pool(name="keep", bufs=1))
-        psum = ctx.enter_context(tc.psum_pool(name="psum", bufs=8))
+        psum = ctx.enter_context(tc.psum_pool(name="psum", bufs=1))
 
         def load_list(src, name):
             tile = keep.tile(list(src.shape), U16, name=name)
@@ -62,16 +62,18 @@ def tile_picked_tokens_codes_one_mixedpair_store_posted_kernel(
         for page in pages:
             nc.vector.memset(page[:], 0.0)
 
-        list1 = load_list(offs, "list1")
-        xw_win = keep.tile([P, T], U16, name="xw_win")
-        nc.sync.dma_start(xw_win[:].bitcast(I32), xt_words[0].bitcast(I32))
-        list2 = load_list(offs2, "list2")
-        ha_t = load_dealt(ha, "ha_t", nc.sync)
+        xs_stage = keep.tile([P, 4, T], U8, name="xs_stage")
+        nc.sync.dma_start(xs_stage[0:4].bitcast(I32), xt_scales[0].rearrange("(q i) c -> i q c", i=4).bitcast(I32))
         ua_rows = ua.rearrange("(p j) f -> p j f", j=PACK)
         ua_t = [keep.tile([P, F], F32, name="ua%d" % j) for j in range(PACK)]
         nc.sync.dma_start(ua_t[0][:], ua_rows[:, 0, :])
-        load_scale_rows(xt_scales, xs_win, nc.sync)
-        for j in range(1, PACK):
+        list1 = load_list(offs, "list1")
+        list2 = load_list(offs2, "list2")
+        ha_t = load_dealt(ha, "ha_t", nc.sync)
+        nc.sync.dma_start(ua_t[1][:], ua_rows[:, 1, :])
+        xw_win = keep.tile([P, T], U16, name="xw_win")
+        nc.sync.dma_start(xw_win[:].bitcast(I32), xt_words[0].bitcast(I32))
+        for j in range(2, PACK):
             nc.sync.dma_start(ua_t[j][:], ua_rows[:, j, :])
         list4 = load_list(offs4, "list4")
         sb_t = load_dealt(sb, "sb_t", nc.sync)
@@ -87,108 +89,124 @@ def tile_picked_tokens_codes_one_mixedpair_store_posted_kernel(
         with nc.allow_non_contiguous_dma(reason="one weight a partition and block"):
             nc.sync.dma_start(so_t[:], so.rearrange("(b p) one -> p (b one)", p=P))
 
-        xw = [keep.tile([P, BANK], U16, name="xw%d" % h, align_bytes=64) for h in range(2)]
-        xs = [keep.tile([P, BANK], U8, name="xs%d" % h, align_bytes=64) for h in range(2)]
-        for h in range(2):
-            nc.vector.tensor_copy(xw[h][:], xw_win[:].indirect(entries(list1, h * BANK, (h + 1) * BANK)))
+        for q in range(4):
+            nc.vector.tensor_copy(xs_win[32 * q : 32 * q + 4, :].bitcast(I32), xs_stage[0:4, q, :].bitcast(I32))
+        xw = [keep.tile([P, BANK], U16, name="xw%d" % h, tag="xw%d" % h, align_bytes=64) for h in range(2)]
+        xs = [keep.tile([P, BANK], U8, name="xs%d" % h, tag="xs%d" % h, align_bytes=64) for h in range(2)]
         for h in range(2):
             nc.vector.tensor_copy(xs[h][:], xs_win[:].indirect(entries(list1, h * BANK, (h + 1) * BANK)))
+        for h in range(2):
+            nc.vector.tensor_copy(xw[h][:], xw_win[:].indirect(entries(list1, h * BANK, (h + 1) * BANK)))
 
         wc = keep.tile([P, PACK, R], BF16, name="wc")
         for j in range(PACK):
-            nc.scalar.activation(out=wc[:, j, :], in_=ua_t[j][:].indirect(list2[:]), func=COPY, scale=ha_t[:, j : j + 1])
+            for lo, hi in [(0, R)] if j < PACK - 1 else [(0, R // 2), (R // 2, R)]:
+                nc.scalar.activation(
+                    out=wc[:, j, lo:hi], in_=ua_t[j][:].indirect(entries(list2, lo, hi)), func=COPY, scale=ha_t[:, j : j + 1]
+                )
 
         wc_dealt = wc[:].rearrange("p j (m t) -> p t m j", t=PACK)
-        wc_woven = [keep.tile([P, P, PACK], BF16, name="wc_woven%d" % t, align_bytes=64) for t in range(PACK)]
-        wc_codes = [keep.tile([P, P], U32, name="wc_codes%d" % t, align_bytes=64) for t in range(PACK)]
+        wc_woven = [keep.tile([P, P, PACK], BF16, name="wc_woven%d" % t, align_bytes=64) for t in range(PACK - 1)]
+        wc_codes = [keep.tile([P, P], U32, name="wc_codes%d" % t, tag="wc_codes%d" % t, align_bytes=64) for t in range(PACK)]
         wc_scales = [keep.tile([P, P], U8, name="wc_scales%d" % t, align_bytes=64) for t in range(PACK)]
-        for t in range(PACK):
-            nc.vector.tensor_copy(wc_woven[t][:], wc_dealt[:, t])
-            nc.vector.quantize_mx(
-                out=wc_codes[t][:].bitcast(FP8X4), scales=wc_scales[t][:],
-                in_=wc_woven[t][:].rearrange("p m j -> p (m j)"),
-            )
-
         a_t = [keep.tile([P, J], F32, name="a%d" % t) for t in range(PACK)]
-        for t in range(PACK):
-            pieces = [(0, 256), (256, 512), (512, 768), (768, 1024)] if t == 0 else [(0, 512), (512, 1024)]
-            for lo, hi in pieces:
-                h, c0, c1 = lo // BANK, lo % BANK, lo % BANK + hi - lo
-                acc = psum.tile([P, BANK], F32, name="acc")
-                nc.tensor.matmul_mx(
-                    out=acc[:, : hi - lo], lhsT=wc_codes[t][:].bitcast(FP8X4), lhsT_scale=wc_scales[t][:],
-                    rhs=xw[h][:, c0:c1].bitcast(FP4X4), rhs_scale=xs[h][:, c0:c1], start=True, stop=True,
-                )
-                if t == 0:
-                    nc.scalar.copy(a_t[t][:, lo:hi], acc[:, : hi - lo])
-                else:
-                    nc.vector.tensor_copy(a_t[t][:, lo:hi], acc[:, : hi - lo])
 
-        vw = keep.tile([P, N], U16, name="vw", align_bytes=64)
-        vsc = keep.tile([P, N], U8, name="vsc", align_bytes=64)
+        def first_product(t, lo, hi, bank):
+            h, c0 = divmod(lo, BANK)
+            acc = psum.tile([P, hi - lo], F32, name="acc", tag="bank%d" % bank)
+            nc.tensor.matmul_mx(
+                out=acc[:], lhsT=wc_codes[t][:].bitcast(FP8X4), lhsT_scale=wc_scales[t][:],
+                rhs=xw[h][:, c0 : c0 + hi - lo].bitcast(FP4X4), rhs_scale=xs[h][:, c0 : c0 + hi - lo], start=True, stop=True,
+            )
+            return acc[:]
+
+        for t in range(PACK):
+            if t == PACK - 1:
+                wc_woven.append(keep.tile([P, P, PACK], BF16, name="wc_woven3", tag="wc_codes0", align_bytes=64))
+            for lo, hi in [(0, P // 2), (P // 2, P)] if t == 0 else [(0, P)]:
+                if t in (1, 2):
+                    nc.scalar.copy(wc_woven[t][:, lo:hi], wc_dealt[:, t, lo:hi])
+                else:
+                    nc.vector.tensor_copy(wc_woven[t][:, lo:hi], wc_dealt[:, t, lo:hi])
+                nc.vector.quantize_mx(
+                    out=wc_codes[t][:, lo:hi].bitcast(FP8X4), scales=wc_scales[t][:, lo:hi],
+                    in_=wc_woven[t][:, lo:hi].rearrange("p m j -> p (m j)"),
+                )
+            if t == 0:
+                for i in range(4):
+                    acc = first_product(0, 256 * i, 256 * (i + 1), i)
+                    if i < 3:
+                        nc.scalar.copy(a_t[0][:, 256 * i : 256 * (i + 1)], acc)
+                    else:
+                        nc.vector.tensor_copy(a_t[0][:, 256 * i : 256 * (i + 1)], acc)
+            elif t == 1:
+                for h in range(2):
+                    nc.vector.tensor_copy(a_t[1][:, h * BANK : (h + 1) * BANK], first_product(1, h * BANK, (h + 1) * BANK, 4 + h))
+        for t, lo, hi, bank in ((3, 0, 512, 0), (2, 0, 512, 6), (2, 512, 768, 7), (3, 512, 1024, 1), (2, 768, 1024, 0)):
+            nc.vector.tensor_copy(a_t[t][:, lo:hi], first_product(t, lo, hi, bank))
+
+        vw = keep.tile([P, N], U16, name="vw", tag="xw1", align_bytes=64)
+        vsc = keep.tile([P, N], U8, name="vsc", tag="xs1", align_bytes=64)
         nc.vector.tensor_copy(vsc[:], vs_s_win[:].indirect(list5[:]))
         nc.vector.tensor_copy(vw[:], vs_w_win[:].indirect(list5[:]))
 
-        shared = [keep.tile([P, O], F32, name="shared%d" % t) for t in range(PACK)]
-        own = [keep.tile([P, O], F32, name="own%d" % t) for t in range(PACK)]
-        hid = keep.tile([P, PACK, O], BF16, name="hid")
+        shared = keep.tile([P, PACK, O], F32, name="shared")
+        own = keep.tile([P, PACK, O], F32, name="own")
         p_t = [keep.tile([P, O], F32, name="p%d" % b) for b in range(2)]
 
         def fetch_shared(t, lo, hi):
-            nc.scalar.activation(out=shared[t][:, lo:hi], in_=a_t[t][:].indirect(entries(list3, lo, hi)), func=COPY, scale=sa_t[:, t : t + 1])
+            nc.scalar.activation(out=shared[:, t, lo:hi], in_=a_t[t][:].indirect(entries(list3, lo, hi)), func=COPY, scale=sa_t[:, t : t + 1])
 
         def fetch_own(t, lo, hi):
-            nc.scalar.activation(out=own[t][:, lo:hi], in_=a_t[t][:].indirect(entries(list4, lo, hi)), func=COPY, scale=sb_t[:, t : t + 1])
+            nc.scalar.activation(out=own[:, t, lo:hi], in_=a_t[t][:].indirect(entries(list4, lo, hi)), func=COPY, scale=sb_t[:, t : t + 1])
 
-        def larger(t, lo, hi):
-            nc.vector.tensor_tensor(hid[:, t, lo:hi], shared[t][:, lo:hi], own[t][:, lo:hi], MAX)
+        sums = {}
 
-        sums = []
-
-        def second_product(lo, hi):
+        def second_product(woven, lo, hi, bank):
             w = hi - lo
-            woven = keep.tile([P, w, PACK], BF16, name="hid_woven%d" % lo, align_bytes=64)
             codes = keep.tile([P, w], U32, name="hid_codes%d" % lo, align_bytes=64)
             scales = keep.tile([P, w], U8, name="hid_scales%d" % lo, align_bytes=64)
-            nc.vector.tensor_copy(woven[:], hid[:, :, lo:hi].rearrange("p t o -> p o t"))
-            nc.vector.quantize_mx(out=codes[:].bitcast(FP8X4), scales=scales[:], in_=woven[:].rearrange("p o t -> p (o t)"))
+            nc.vector.tensor_tensor(
+                woven.rearrange("p (c i) t -> p c t i", i=4),
+                shared[:, :, lo:hi].rearrange("p t (c i) -> p c t i", i=4),
+                own[:, :, lo:hi].rearrange("p t (c i) -> p c t i", i=4),
+                MAX,
+            )
+            nc.vector.quantize_mx(out=codes[:].bitcast(FP8X4), scales=scales[:], in_=woven.rearrange("p o t -> p (o t)"))
             for b in range(2):
-                acc = psum.tile([P, BANK], F32, name="acc")
+                acc = psum.tile([P, w], F32, name="acc", tag="bank%d" % (bank + b))
                 nc.tensor.matmul_mx(
                     out=acc[:, :w], lhsT=vw[:, b * P : (b + 1) * P].bitcast(FP4X4), lhsT_scale=vsc[:, b * P : (b + 1) * P],
                     rhs=codes[:].bitcast(FP8X4), rhs_scale=scales[:], start=True, stop=True,
                 )
-                sums.append((b, lo, hi, acc))
+                sums[b, lo, hi] = acc
 
         for t in range(2):
             fetch_own(t, 0, O)
             fetch_shared(t, 0, O)
-            larger(t, 0, O)
-        for t in range(2, 4):
+        for t in (3, 2):
             fetch_own(t, 0, 256)
             fetch_shared(t, 0, 256)
-            larger(t, 0, 256)
-        second_product(0, 256)
-        fetch_own(2, 256, 512)
-        fetch_shared(2, 256, 512)
-        larger(2, 256, 512)
-        fetch_own(3, 256, 512)
+        first_half = keep.tile([P, 256, PACK], BF16, name="first_half", tag="hid_woven", align_bytes=64)
+        second_product(first_half[:], 0, 256, 2)
+        for t in (3, 2):
+            fetch_own(t, 256, 512)
+        second_half = keep.tile([P, 256, PACK], BF16, name="second_half", tag="hid_woven", align_bytes=64)
         for lo in (256, 384):
-            fetch_shared(3, lo, lo + 128)
-            larger(3, lo, lo + 128)
-            second_product(lo, lo + 128)
+            for t in (3, 2):
+                fetch_shared(t, lo, lo + 128)
+            second_product(second_half[:, lo - 256 : lo - 128], lo, lo + 128, lo // 64)
 
-        for b in range(2):
-            for bb, lo, hi, acc in sums:
-                if bb == b and hi < O:
-                    nc.scalar.copy(p_t[b][:, lo:hi], acc[:, : hi - lo])
+        def empty(b, lo, hi):
+            nc.scalar.copy(p_t[b][:, lo:hi], sums[b, lo, hi][:, : hi - lo])
+
+        for lo, hi in ((0, 256), (256, 384)):
+            for b in range(2):
+                empty(b, lo, hi)
         m0 = [keep.tile([P, U], F32, name="m0_%d" % b) for b in range(2)]
         for b in range(2):
-            for bb, lo, hi, acc in sums:
-                if bb == b and hi == O:
-                    nc.scalar.copy(p_t[b][:, lo:hi], acc[:, : hi - lo])
-            cuts = [(0, 128), (128, 256)] if b == 0 else [(0, 256)]
-            for lo, hi in cuts:
-                nc.scalar.activation(out=m0[b][:, lo:hi], in_=p_t[b][:].indirect(entries(list6, lo, hi)), func=COPY, scale=so_t[:, b : b + 1])
-                nc.vector.tensor_copy(pages[b][:].indirect(entries(list7, lo, hi)), m0[b][:, lo:hi])
+            nc.vector.tensor_copy(p_t[b][:, 384:512], sums[b, 384, 512][:, :128])
+        for b in range(2):
+            nc.scalar.activation(out=m0[b][:], in_=p_t[b][:].indirect(list6[:]), func=COPY, scale=so_t[:, b : b + 1])
+            nc.vector.tensor_copy(pages[b][:].indirect(list7[:]), m0[b][:])
             nc.sync.dma_start(out[b * P : (b + 1) * P, :], pages[b][:])

from contextlib import ExitStack

import concourse.mybir as mybir

K, J, R, T, F, O, N, S, U, E = 512, 1024, 512, 2048, 1024, 512, 256, 1024, 256, 1024
FLOPS = 2 * K * R * J + 2 * R * N * O

F32 = mybir.dt.float32
BF16 = mybir.dt.bfloat16
I32 = mybir.dt.int32
U32 = mybir.dt.uint32
U16 = mybir.dt.uint16
U8 = mybir.dt.uint8
FP8X4 = mybir.dt.float8_e4m3fn_x4
FP4X4 = mybir.dt.float4_e2m1fn_x4
COPY = mybir.ActivationFunctionType.Copy
MAX = mybir.AluOpType.max

P = 128
PACK = 4
BANK = 512
LIST = 16


def entries(offsets, lo, hi):
    return offsets[:, lo // LIST : hi // LIST]


def tile_picked_tokens_codes_one_mixedpair_store_posted_kernel(
    tc, xt_words, xt_scales, ua, ha, sa, sb, vs_words, vs_scales, so,
    offs, offs2, offs3, offs4, offs5, offs6, offs7, out,
):
    nc = tc.nc
    with ExitStack() as ctx:
        keep = ctx.enter_context(tc.tile_pool(name="keep", bufs=1))
        psum = ctx.enter_context(tc.psum_pool(name="psum", bufs=1))

        def load_list(src, name):
            tile = keep.tile(list(src.shape), U16, name=name)
            nc.sync.dma_start(tile[:], src)
            return tile

        def load_scale_rows(src, window, queue):
            for q in range(4):
                queue.dma_start(window[32 * q : 32 * q + 4, :].bitcast(I32), src[0, 4 * q : 4 * q + 4, :].bitcast(I32))

        def load_dealt(src, name, queue):
            tile = keep.tile([P, PACK], F32, name=name)
            queue.dma_start(tile[:], src.rearrange("(p j) one -> p (j one)", j=PACK))
            return tile

        idle_in = keep.tile([P, 1], F32, name="idle_in")
        idle_out = keep.tile([P, 1], F32, name="idle_out")
        nc.gpsimd.memset(idle_in[:], 0.0)
        nc.scalar.activation(out=idle_out[:], in_=idle_in[:], func=COPY)

        xs_win = keep.tile([P, T], U8, name="xs_win")
        nc.vector.memset(xs_win[:].bitcast(I32), 0)
        vs_s_win = keep.tile([P, S], U8, name="vs_s_win")
        nc.vector.memset(vs_s_win[:].bitcast(I32), 0)
        pages = [keep.tile([P, E], F32, name="page%d" % b) for b in range(2)]
        for page in pages:
            nc.vector.memset(page[:], 0.0)

        xs_stage = keep.tile([P, 4, T], U8, name="xs_stage")
        nc.sync.dma_start(xs_stage[0:4].bitcast(I32), xt_scales[0].rearrange("(q i) c -> i q c", i=4).bitcast(I32))
        ua_rows = ua.rearrange("(p j) f -> p j f", j=PACK)
        ua_t = [keep.tile([P, F], F32, name="ua%d" % j) for j in range(PACK)]
        nc.sync.dma_start(ua_t[0][:], ua_rows[:, 0, :])
        list1 = load_list(offs, "list1")
        list2 = load_list(offs2, "list2")
        ha_t = load_dealt(ha, "ha_t", nc.sync)
        nc.sync.dma_start(ua_t[1][:], ua_rows[:, 1, :])
        xw_win = keep.tile([P, T], U16, name="xw_win")
        nc.sync.dma_start(xw_win[:].bitcast(I32), xt_words[0].bitcast(I32))
        for j in range(2, PACK):
            nc.sync.dma_start(ua_t[j][:], ua_rows[:, j, :])
        list4 = load_list(offs4, "list4")
        sb_t = load_dealt(sb, "sb_t", nc.sync)
        list3 = load_list(offs3, "list3")
        sa_t = load_dealt(sa, "sa_t", nc.sync)
        list5 = load_list(offs5, "list5")
        vs_w_win = keep.tile([P, S], U16, name="vs_w_win")
        nc.sync.dma_start(vs_w_win[:].bitcast(I32), vs_words[0].bitcast(I32))
        load_scale_rows(vs_scales, vs_s_win, nc.sync)
        list6 = load_list(offs6, "list6")
        list7 = load_list(offs7, "list7")
        so_t = keep.tile([P, 2], F32, name="so_t")
        with nc.allow_non_contiguous_dma(reason="one weight a partition and block"):
            nc.sync.dma_start(so_t[:], so.rearrange("(b p) one -> p (b one)", p=P))

        for q in range(4):
            nc.vector.tensor_copy(xs_win[32 * q : 32 * q + 4, :].bitcast(I32), xs_stage[0:4, q, :].bitcast(I32))
        xw = [keep.tile([P, BANK], U16, name="xw%d" % h, tag="xw%d" % h, align_bytes=64) for h in range(2)]
        xs = [keep.tile([P, BANK], U8, name="xs%d" % h, tag="xs%d" % h, align_bytes=64) for h in range(2)]
        for h in range(2):
            nc.vector.tensor_copy(xs[h][:], xs_win[:].indirect(entries(list1, h * BANK, (h + 1) * BANK)))
        for h in range(2):
            nc.vector.tensor_copy(xw[h][:], xw_win[:].indirect(entries(list1, h * BANK, (h + 1) * BANK)))

        wc = keep.tile([P, PACK, R], BF16, name="wc")
        for j in range(PACK):
            for lo, hi in [(0, R)] if j < PACK - 1 else [(0, R // 2), (R // 2, R)]:
                nc.scalar.activation(
                    out=wc[:, j, lo:hi], in_=ua_t[j][:].indirect(entries(list2, lo, hi)), func=COPY, scale=ha_t[:, j : j + 1]
                )

        wc_dealt = wc[:].rearrange("p j (m t) -> p t m j", t=PACK)
        wc_woven = [keep.tile([P, P, PACK], BF16, name="wc_woven%d" % t, align_bytes=64) for t in range(PACK - 1)]
        wc_codes = [keep.tile([P, P], U32, name="wc_codes%d" % t, tag="wc_codes%d" % t, align_bytes=64) for t in range(PACK)]
        wc_scales = [keep.tile([P, P], U8, name="wc_scales%d" % t, align_bytes=64) for t in range(PACK)]
        a_t = [keep.tile([P, J], F32, name="a%d" % t) for t in range(PACK)]

        def first_product(t, lo, hi, bank):
            h, c0 = divmod(lo, BANK)
            acc = psum.tile([P, hi - lo], F32, name="acc", tag="bank%d" % bank)
            nc.tensor.matmul_mx(
                out=acc[:], lhsT=wc_codes[t][:].bitcast(FP8X4), lhsT_scale=wc_scales[t][:],
                rhs=xw[h][:, c0 : c0 + hi - lo].bitcast(FP4X4), rhs_scale=xs[h][:, c0 : c0 + hi - lo], start=True, stop=True,
            )
            return acc[:]

        for t in range(PACK):
            if t == PACK - 1:
                wc_woven.append(keep.tile([P, P, PACK], BF16, name="wc_woven3", tag="wc_codes0", align_bytes=64))
            for lo, hi in [(0, P // 2), (P // 2, P)] if t == 0 else [(0, P)]:
                if t in (1, 2):
                    nc.scalar.copy(wc_woven[t][:, lo:hi], wc_dealt[:, t, lo:hi])
                else:
                    nc.vector.tensor_copy(wc_woven[t][:, lo:hi], wc_dealt[:, t, lo:hi])
                nc.vector.quantize_mx(
                    out=wc_codes[t][:, lo:hi].bitcast(FP8X4), scales=wc_scales[t][:, lo:hi],
                    in_=wc_woven[t][:, lo:hi].rearrange("p m j -> p (m j)"),
                )
            if t == 0:
                for i in range(4):
                    acc = first_product(0, 256 * i, 256 * (i + 1), i)
                    if i < 3:
                        nc.scalar.copy(a_t[0][:, 256 * i : 256 * (i + 1)], acc)
                    else:
                        nc.vector.tensor_copy(a_t[0][:, 256 * i : 256 * (i + 1)], acc)
            elif t == 1:
                for h in range(2):
                    nc.vector.tensor_copy(a_t[1][:, h * BANK : (h + 1) * BANK], first_product(1, h * BANK, (h + 1) * BANK, 4 + h))
        for t, lo, hi, bank in ((3, 0, 512, 0), (2, 0, 512, 6), (2, 512, 768, 7), (3, 512, 1024, 1), (2, 768, 1024, 0)):
            nc.vector.tensor_copy(a_t[t][:, lo:hi], first_product(t, lo, hi, bank))

        vw = keep.tile([P, N], U16, name="vw", tag="xw1", align_bytes=64)
        vsc = keep.tile([P, N], U8, name="vsc", tag="xs1", align_bytes=64)
        nc.vector.tensor_copy(vsc[:], vs_s_win[:].indirect(list5[:]))
        nc.vector.tensor_copy(vw[:], vs_w_win[:].indirect(list5[:]))

        shared = keep.tile([P, PACK, O], F32, name="shared")
        own = keep.tile([P, PACK, O], F32, name="own")
        p_t = [keep.tile([P, O], F32, name="p%d" % b) for b in range(2)]

        def fetch_shared(t, lo, hi):
            nc.scalar.activation(out=shared[:, t, lo:hi], in_=a_t[t][:].indirect(entries(list3, lo, hi)), func=COPY, scale=sa_t[:, t : t + 1])

        def fetch_own(t, lo, hi):
            nc.scalar.activation(out=own[:, t, lo:hi], in_=a_t[t][:].indirect(entries(list4, lo, hi)), func=COPY, scale=sb_t[:, t : t + 1])

        sums = {}

        def second_product(woven, lo, hi, bank):
            w = hi - lo
            codes = keep.tile([P, w], U32, name="hid_codes%d" % lo, align_bytes=64)
            scales = keep.tile([P, w], U8, name="hid_scales%d" % lo, align_bytes=64)
            nc.vector.tensor_tensor(
                woven.rearrange("p (c i) t -> p c t i", i=4),
                shared[:, :, lo:hi].rearrange("p t (c i) -> p c t i", i=4),
                own[:, :, lo:hi].rearrange("p t (c i) -> p c t i", i=4),
                MAX,
            )
            nc.vector.quantize_mx(out=codes[:].bitcast(FP8X4), scales=scales[:], in_=woven.rearrange("p o t -> p (o t)"))
            for b in range(2):
                acc = psum.tile([P, w], F32, name="acc", tag="bank%d" % (bank + b))
                nc.tensor.matmul_mx(
                    out=acc[:, :w], lhsT=vw[:, b * P : (b + 1) * P].bitcast(FP4X4), lhsT_scale=vsc[:, b * P : (b + 1) * P],
                    rhs=codes[:].bitcast(FP8X4), rhs_scale=scales[:], start=True, stop=True,
                )
                sums[b, lo, hi] = acc

        for t in range(2):
            fetch_own(t, 0, O)
            fetch_shared(t, 0, O)
        for t in (3, 2):
            fetch_own(t, 0, 256)
            fetch_shared(t, 0, 256)
        first_half = keep.tile([P, 256, PACK], BF16, name="first_half", tag="hid_woven", align_bytes=64)
        second_product(first_half[:], 0, 256, 2)
        for t in (3, 2):
            fetch_own(t, 256, 512)
        second_half = keep.tile([P, 256, PACK], BF16, name="second_half", tag="hid_woven", align_bytes=64)
        for lo in (256, 384):
            for t in (3, 2):
                fetch_shared(t, lo, lo + 128)
            second_product(second_half[:, lo - 256 : lo - 128], lo, lo + 128, lo // 64)

        def empty(b, lo, hi):
            nc.scalar.copy(p_t[b][:, lo:hi], sums[b, lo, hi][:, : hi - lo])

        for lo, hi in ((0, 256), (256, 384)):
            for b in range(2):
                empty(b, lo, hi)
        m0 = [keep.tile([P, U], F32, name="m0_%d" % b) for b in range(2)]
        for b in range(2):
            nc.vector.tensor_copy(p_t[b][:, 384:512], sums[b, 384, 512][:, :128])
        for b in range(2):
            nc.scalar.activation(out=m0[b][:], in_=p_t[b][:].indirect(list6[:]), func=COPY, scale=so_t[:, b : b + 1])
            nc.vector.tensor_copy(pages[b][:].indirect(list7[:]), m0[b][:])
            nc.sync.dma_start(out[b * P : (b + 1) * P, :], pages[b][:])
